import numpy as np
import ml_dtypes


def mxq(x, axis, fmt="e4m3"):
    dtype, down = {"e4m3": (ml_dtypes.float8_e4m3fn, 7), "e5m2": (ml_dtypes.float8_e5m2, 14)}[fmt]
    v = np.moveaxis(np.asarray(x, np.float32).astype(ml_dtypes.bfloat16).astype(np.float64), axis, -1)
    blocks = v.reshape(v.shape[:-1] + (-1, 32))
    amax = np.abs(blocks).max(-1, keepdims=True)
    byte = np.maximum(np.where(amax > 0, np.frexp(amax)[1] - 1 + 127, 0) - down, 1)
    scale = np.exp2(byte - 127.0)
    codes = (blocks / scale).astype(np.float32).astype(dtype).astype(np.float64)
    return np.moveaxis((codes * scale).reshape(v.shape), -1, axis)


WIDE = False


def mx_kscale(k):
    if not WIDE:
        return np.ones(k)
    levels = np.array([10, -10, 5, -5, 0])
    if k % 512:
        return np.exp2(np.random.permutation(np.resize(levels, k // 32))).repeat(32)
    a = np.empty((k // 512, 16))
    for p in range(k // 512):
        a[p, :8] = np.random.permutation(np.resize(levels, 8))
        for g in range(8):
            far = levels[np.abs(levels - a[p, g]) >= 10]
            a[p, g + 8] = far[np.random.randint(len(far))]
    return np.exp2(a.ravel()).repeat(32)


BF16 = ml_dtypes.bfloat16


def bf(x):
    return np.asarray(x, np.float32).astype(BF16)


def f64(x):
    return np.asarray(x).astype(np.float64)


T, D, F, S, C = 1024, 1024, 1024, 512, 16

GELU_A = np.sqrt(2.0 / np.pi)
GELU_B = 0.044715


def gelu(z):
    return 0.5 * z * (1.0 + np.tanh(GELU_A * (z + GELU_B * z * z * z)))


def draw0():
    s = mx_kscale(D)
    ts = mx_kscale(T)
    te = mx_kscale(T)
    return {"x": bf(np.random.standard_normal((T, D)) * s),
            "ws": bf(np.random.standard_normal((D, F)) / np.sqrt(D) / s[:, None]),
            "we": bf(np.random.standard_normal((D, F)) / np.sqrt(D) / s[:, None]),
            "bs": bf(0.3 * np.random.standard_normal(F)),
            "be": bf(0.3 * np.random.standard_normal(F)),
            "gs": bf(np.random.uniform(0.5, 1.5, T) * ts),
            "ge": bf(np.random.uniform(0.5, 1.5, T) * te),
            "ps": bf(np.random.standard_normal((S, T)) / np.sqrt(T) / ts),
            "pe": bf(np.random.standard_normal((S, T)) / np.sqrt(T) / te),
            "mix": bf(1.0 + 0.1 * np.random.standard_normal(F)),
            "v": bf(np.random.standard_normal(F) / np.sqrt(F // C)),
            "d": bf(0.3 * np.random.standard_normal(C))}


def core(x, ws, we, bs, be, gs, ge, ps, pe, mix, v, d):
    xq = mxq(f64(x), 1, "e4m3")
    hs = gelu((xq @ mxq(f64(ws), 0, "e4m3")) + f64(bs)) * f64(gs)[:, None]
    he = gelu((xq @ mxq(f64(we), 0, "e4m3")) + f64(be)) * f64(ge)[:, None]
    a = mxq(f64(ps), 1, "e4m3") @ mxq(hs, 0, "e4m3")
    b = mxq(f64(pe), 1, "e4m3") @ mxq(he, 0, "e4m3")
    emb = a + b + f64(mix) * a * b
    score = (emb * f64(v)).reshape(S, C, F // C).sum(axis=2) + f64(d)
    return emb, score


def e4m3fn_bytes(y):
    return np.clip(np.asarray(y, np.float64), -448.0, 448.0).astype(np.float32).astype(ml_dtypes.float8_e4m3fn).view(np.uint8)


def e4m3fn_values(b):
    return np.asarray(b, np.uint8).view(ml_dtypes.float8_e4m3fn).astype(np.float64)


def setup_inputs():
    d = draw0()
    x0 = np.asarray(d['x']).astype(np.float64)
    s = (np.max(np.abs(x0), axis=(0,), keepdims=True) / 448.0).astype(np.float32)
    out = {}
    for k, v in d.items():
        if k == 'x':
            out['x_bytes'] = e4m3fn_bytes(x0 / s.astype(np.float64))
            out['x_scale'] = s
        else:
            out[k] = v
    return out


def reference(x_bytes, x_scale, ws, we, bs, be, gs, ge, ps, pe, mix, v, d):
    return core(e4m3fn_values(x_bytes) * x_scale.astype(np.float64), ws, we, bs, be, gs, ge, ps, pe, mix, v, d)

from contextlib import ExitStack

import concourse.mybir as mybir
from concourse.masks import make_identity

T, D, F, S, C = 1024, 1024, 1024, 512, 16
FLOPS = 2 * 2 * T * D * F + 2 * 2 * S * T * F

F32 = mybir.dt.float32
BF16 = mybir.dt.bfloat16
U32 = mybir.dt.uint32
U8 = mybir.dt.uint8
FP8 = mybir.dt.float8_e4m3fn
FP8X4 = mybir.dt.float8_e4m3fn_x4
ACT = mybir.ActivationFunctionType
ALU = mybir.AluOpType

P = 128
NI = F // P
NR = 2 * NI
WCH = 256


def tile_endpoint_span_scoring_f4_kernel(
    tc, x_bytes, x_scale, ws, we, bs, be, gs, ge, ps, pe, mix, v, d, out_0, out_1
):
    nc = tc.nc
    with ExitStack() as ctx:
        keep = ctx.enter_context(tc.tile_pool(name="keep", bufs=1))
        stage = ctx.enter_context(tc.tile_pool(name="stage", bufs=3))
        zpool = ctx.enter_context(tc.psum_pool(name="zpool", bufs=2))
        tpool = ctx.enter_context(tc.psum_pool(name="tpool", bufs=3))
        apool = ctx.enter_context(tc.psum_pool(name="apool", bufs=2))
        bpool = ctx.enter_context(tc.psum_pool(name="bpool", bufs=1))

        ident = keep.tile([P, P], F32, name="ident")
        make_identity(nc, ident[:])

        xb = [keep.tile([P, 4, D], U8, name=f"xb{h}", align_bytes=64) for h in range(2)]
        xw = [keep.tile([P, 4, D], BF16, name=f"xw{h}", align_bytes=64) for h in range(2)]
        xs = keep.tile([P, 2, 4], F32, name="xs")
        xcodes = keep.tile([P, 2, T], U32, name="xcodes", align_bytes=64)
        xscales = keep.tile([P, 2, T], U8, name="xscales", align_bytes=64)
        praw = [keep.tile([P, 4, T], BF16, name=f"praw{e}", align_bytes=64) for e in range(2)]
        pcodes = [keep.tile([P, 2, S], U32, name=f"pcodes{e}", align_bytes=64) for e in range(2)]
        pscales = [keep.tile([P, 2, S], U8, name=f"pscales{e}", align_bytes=64) for e in range(2)]
        wraw = [
            [keep.tile([P, 2, 4, WCH], BF16, name=f"wraw{e}_{c}", align_bytes=64) for c in range(F // WCH)]
            for e in range(2)
        ]
        sal = [keep.tile([P, 2, 4, 4], BF16, name=f"sal{e}") for e in range(2)]
        rows = keep.tile([P, P], BF16, name="rows")
        rows32 = keep.tile([P, P], F32, name="rows32")
        cols = keep.tile([P, 4, NI], F32, name="cols")
        vmat = keep.tile([P, NI, 2], F32, name="vmat")
        dt_ = keep.tile([P, C], BF16, name="dt_")
        score = keep.tile([P, 4, C], F32, name="score")
        warm = keep.tile([P, 1], F32, name="warm")

        xv = x_bytes.rearrange("(h p j) k -> h p j k", h=2, p=P, j=4)
        wv = [w.rearrange("(g p j) f -> g p j f", g=2, p=P, j=4) for w in (ws, we)]
        pv = [q.rearrange("(st r) t -> r st t", r=P) for q in (ps, pe)]

        def load_w(e, c):
            for g in range(2):
                nc.sync.dma_start(out=wraw[e][c][:, g, :, :], in_=wv[e][g][:, :, c * WCH : (c + 1) * WCH])

        nc.vector.memset(rows[:], 0.0)
        nc.sync.dma_start(out=xb[0][:, 0:2, :], in_=xv[0][:, 0:2, :])
        nc.sync.dma_start(out=xb[0][:, 2:4, :], in_=xv[0][:, 2:4, :])
        nc.sync.dma_start(out=xs[:], in_=x_scale.rearrange("o (g p t) -> p (o g) t", p=P, t=4))
        for q, vec in enumerate((bs, be, mix, v)):
            nc.gpsimd.dma_start(out=rows[NI * q : NI * (q + 1), :], in_=vec.rearrange("(i f) -> i f", f=P))
        for e, gv in enumerate((gs, ge)):
            nc.gpsimd.dma_start(out=sal[e][:, :, 0, :], in_=gv.rearrange("(h m j) -> m h j", h=2, j=4))
        nc.gpsimd.dma_start(out=dt_[:], in_=d.partition_broadcast(P))

        def load_p(e):
            for k in range(2):
                nc.sync.dma_start(out=praw[e][:, 2 * k : 2 * k + 2, :], in_=pv[e][:, 2 * k : 2 * k + 2, :])

        load_p(0)
        load_w(0, 0)
        nc.sync.dma_start(out=xb[1][:], in_=xv[1])
        load_w(1, 0)
        load_p(1)
        for c in range(1, F // WCH):
            load_w(0, c)
            load_w(1, c)

        nc.vector.memset(warm[:], 0.0)
        nc.scalar.activation(out=warm[:], in_=warm[:], func=ACT.Gelu_apprx_tanh)

        def cast_x(eng, h, j):
            src = xb[h][:, j, :].bitcast(FP8)
            if eng is nc.scalar:
                nc.scalar.copy(out=xw[h][:, j, :], in_=src)
            else:
                nc.vector.tensor_copy(out=xw[h][:, j, :], in_=src)

        def words_t(tp, src_words, u, col, base):
            nc.tensor.transpose(tp[:, u, col : col + P], src_words[:, base + u : base + 256 : 2], ident[:])

        def t_x(h, g, jp):
            tp = tpool.tile([P, 2, 256], F32, name="tp")
            for jj in range(2):
                w = xw[h][:, 2 * jp + jj, :].bitcast(F32)
                for u in range(2):
                    words_t(tp, w, u, P * jj, 256 * g)
            return tp

        def prod_x(tp, h, g, xg, jp):
            nc.vector.tensor_tensor(
                out=xg[:, 256 * jp : 256 * (jp + 1), :].rearrange("p r (u e) -> p r u e", e=2),
                in0=tp[:].rearrange("p u r -> p (u r)").bitcast(BF16).rearrange("p (u r e) -> p r u e", u=2, e=2),
                in1=xs[:, g, :].unsqueeze(1).to_broadcast([P, 256, 4]).rearrange("p r (u e) -> p r u e", e=2),
                op=ALU.mult,
            )

        def quant_x(h, g, xg):
            nc.vector.quantize_mx(
                out=xcodes[:, g, 512 * h : 512 * (h + 1)].bitcast(FP8X4),
                scales=xscales[:, g, 512 * h : 512 * (h + 1)],
                in_=xg[:].rearrange("p r q -> p (r q)"),
            )

        def t_p(e, h, sp):
            tp = zpool.tile([P, 2, 256], F32, name="z")
            for ss in range(2):
                w = praw[e][:, 2 * sp + ss, :].bitcast(F32)
                for u in range(2):
                    words_t(tp, w, u, P * ss, 256 * h)
            return tp

        def out_p(tp, pg, sp):
            nc.scalar.copy(
                out=pg[:, 256 * sp : 256 * (sp + 1), :].rearrange("p r q -> p (r q)").bitcast(F32).rearrange("p (r u) -> p r u", u=2),
                in_=tp[:].rearrange("p u r -> p r u"),
            )

        def quant_p(e, h, pg):
            nc.vector.quantize_mx(
                out=pcodes[e][:, h, :].bitcast(FP8X4),
                scales=pscales[e][:, h, :],
                in_=pg[:].rearrange("p r q -> p (r q)"),
            )

        wg, wq, z, gl, tph, hg, hq, av, bv, tv, uv, ev, tpe, tps = ({} for _ in range(14))

        def inter_w(r):
            i, e = divmod(r, 2)
            c, o = divmod(i * P, WCH)
            wg[r] = stage.tile([P, 2, P, 4], BF16, name="wg", align_bytes=64, bufs=4)
            nc.scalar.copy(out=wg[r][:], in_=wraw[e][c][:, :, :, o : o + P].rearrange("p g t f -> p g f t"))

        def quant_w(r):
            cod = stage.tile([P, 2, P], U32, name="wcod", align_bytes=64, bufs=5)
            sca = stage.tile([P, 2, P], U8, name="wsca", align_bytes=64, bufs=5)
            nc.vector.quantize_mx(
                out=cod[:].rearrange("p g f -> p (g f)").bitcast(FP8X4),
                scales=sca[:].rearrange("p g f -> p (g f)"),
                in_=wg.pop(r)[:].rearrange("p g f q -> p (g f q)"),
            )
            wq[r] = (cod, sca)

        def mm1(r, h):
            cod, sca = wq[r]
            zt = zpool.tile([P, 512], F32, name="z")
            for g in range(2):
                nc.tensor.matmul_mx(
                    out=zt[:],
                    lhsT=cod[:, g, :].bitcast(FP8X4),
                    lhsT_scale=sca[:, g, :],
                    rhs=xcodes[:, g, 512 * h : 512 * (h + 1)].bitcast(FP8X4),
                    rhs_scale=xscales[:, g, 512 * h : 512 * (h + 1)],
                    start=(g == 0),
                    stop=(g == 1),
                )
            z[r, h] = zt

        def gelu(r, h):
            i, e = divmod(r, 2)
            gl[r, h] = stage.tile([P, 512], F32, name="gl", bufs=4)
            nc.scalar.activation(
                out=gl[r, h][:], in_=z.pop((r, h))[:], func=ACT.Gelu_apprx_tanh, bias=cols[:, e, i : i + 1]
            )

        def t_h(r, h):
            tp = tpool.tile([P, 2, 256], F32, name="tp")
            flat = tp[:].rearrange("p u r -> p (u r)")
            src = gl.pop((r, h))
            for j in range(4):
                nc.tensor.transpose(flat[:, P * j : P * (j + 1)], src[:, P * j : P * (j + 1)], ident[:])
            tph[r, h] = flat

        def mult_h(r, h):
            e = r % 2
            if h == 0:
                hg[r] = stage.tile([P, 2, P, 4], BF16, name="hg", align_bytes=64)
            nc.vector.tensor_tensor(
                out=hg[r][:, h, :, :],
                in0=tph.pop((r, h)).rearrange("p (j f) -> p f j", j=4),
                in1=sal[e][:, h, 0, :].unsqueeze(1).to_broadcast([P, P, 4]),
                op=ALU.mult,
            )

        def quant_h(r):
            cod = stage.tile([P, 2, P], U32, name="hcod", align_bytes=64, bufs=4)
            sca = stage.tile([P, 2, P], U8, name="hsca", align_bytes=64, bufs=4)
            nc.vector.quantize_mx(
                out=cod[:].rearrange("p g f -> p (g f)").bitcast(FP8X4),
                scales=sca[:].rearrange("p g f -> p (g f)"),
                in_=hg.pop(r)[:].rearrange("p g f q -> p (g f q)"),
            )
            hq[r] = (cod, sca)

        def mm2(r):
            i, e = divmod(r, 2)
            cod, sca = hq.pop(r)
            if e == 0:
                o = apool.tile([P, S], F32, name="a")
                av[i] = o
            else:
                o = bpool.tile([P, S], F32, name="b")
                bv[i] = o
            for h in range(2):
                nc.tensor.matmul_mx(
                    out=o[:],
                    lhsT=cod[:, h, :].bitcast(FP8X4),
                    lhsT_scale=sca[:, h, :],
                    rhs=pcodes[e][:, h, :].bitcast(FP8X4),
                    rhs_scale=pscales[e][:, h, :],
                    start=(h == 0),
                    stop=(h == 1),
                )

        def emb_t(i):
            tv[i] = stage.tile([P, S], F32, name="tv")
            nc.scalar.activation(out=tv[i][:], in_=av[i][:], func=ACT.Identity, bias=1.0, scale=cols[:, 2, i : i + 1])

        def emb_u(i):
            uv[i] = stage.tile([P, S], F32, name="uv")
            nc.vector.tensor_tensor(out=uv[i][:], in0=bv.pop(i)[:], in1=tv.pop(i)[:], op=ALU.mult)

        def emb_e(i):
            ev[i] = stage.tile([P, S], F32, name="ev")
            nc.vector.tensor_tensor(out=ev[i][:], in0=av.pop(i)[:], in1=uv.pop(i)[:], op=ALU.add)

        def t_emb(i):
            tp = tpool.tile([P, 2, 256], F32, name="tp")
            flat = tp[:].rearrange("p u r -> p (u r)")
            for st in range(4):
                nc.tensor.transpose(flat[:, P * st : P * (st + 1)], ev[i][:, P * st : P * (st + 1)], ident[:])
            tpe[i] = flat
            sc = bpool.tile([P, S], F32, name="b")
            for st in range(4):
                nc.tensor.matmul(
                    out=sc[:, 2 * st : 2 * st + 2],
                    lhsT=ev[i][:, P * st : P * (st + 1)],
                    rhs=vmat[:, i, :],
                    start=True,
                    stop=True,
                )
            tps[i] = sc
            ev.pop(i)

        def out_score(i):
            nc.vector.tensor_tensor(
                out=score[:, :, 2 * i : 2 * i + 2],
                in0=tps.pop(i)[:, 0:8].rearrange("p (st c) -> p st c", c=2),
                in1=dt_[:, 2 * i : 2 * i + 2].unsqueeze(1).to_broadcast([P, 4, 2]),
                op=ALU.add,
            )

        def out_emb(i):
            eo = stage.tile([P, S], F32, name="eo")
            nc.scalar.copy(out=eo[:], in_=tpe.pop(i))
            nc.sync.dma_start(
                out=out_0.rearrange("(st r) f -> r st f", r=P)[:, :, P * i : P * (i + 1)],
                in_=eo[:].rearrange("p (st f) -> p st f", st=4),
            )

        with tc.manual_schedule():
            def x_half(h, engs):
                for j in range(4):
                    cast_x(engs[j], h, j)
                xg = [stage.tile([P, 512, 4], BF16, name=f"xg{g}", align_bytes=64) for g in range(2)]
                for jp in range(2):
                    tps_ = [t_x(h, g, jp) for g in range(2)]
                    for g in range(2):
                        prod_x(tps_[g], h, g, xg[g], jp)
                return xg

            def p_half(e, h):
                pg = stage.tile([P, S, 4], BF16, name="pg", align_bytes=64, bufs=4)
                for sp in range(2):
                    out_p(t_p(e, h, sp), pg, sp)
                return pg

            xg = x_half(0, (nc.scalar, nc.vector, nc.scalar, nc.vector))
            inter_w(0)
            pgs = [p_half(0, h) for h in range(2)]
            quant_x(0, 0, xg[0])
            nc.vector.tensor_copy(out=rows32[:], in_=rows[:])
            quant_x(0, 1, xg[1])
            tpv = tpool.tile([P, 2, 256], F32, name="tp")
            nc.tensor.transpose(tpv[:, 0, 0:P], rows32[:], ident[:])
            quant_w(0)
            mm1(0, 0)
            nc.vector.memset(vmat[:], 0.0)
            nc.vector.tensor_copy(out=cols[:].rearrange("p q i -> p (q i)"), in_=tpv[:, 0, 0:32])
            xg = x_half(1, (nc.scalar,) * 4)
            gelu(0, 0)
            inter_w(1)
            nc.vector.tensor_copy(out=vmat[0:64, :, 0], in_=cols[0:64, 3, :])
            quant_x(1, 0, xg[0])
            nc.vector.tensor_copy(out=vmat[64:128, :, 1], in_=cols[64:128, 3, :])
            quant_x(1, 1, xg[1])
            quant_w(1)
            mm1(0, 1)
            gelu(0, 1)
            quant_p(0, 0, pgs[0])
            inter_w(2)
            quant_p(0, 1, pgs[1])
            inter_w(3)
            quant_w(2)

            for n in range(1, NR + 6):
                if n < NR:
                    mm1(n, 0)
                    mm1(n, 1)
                if 0 <= n - 2 < NR:
                    quant_h(n - 2)
                if 0 <= n - 3 < NR:
                    mm2(n - 3)
                i, odd = divmod(n - 5, 2)
                emb = odd == 0 and 0 <= i < NI
                if emb:
                    emb_u(i)
                if 0 <= n - 1 < NR:
                    t_h(n - 1, 0)
                    t_h(n - 1, 1)
                if n < NR:
                    gelu(n, 0)
                    gelu(n, 1)
                if 0 <= n - 1 < NR:
                    mult_h(n - 1, 0)
                if emb:
                    emb_e(i)
                    t_emb(i)
                if 0 <= n - 1 < NR:
                    mult_h(n - 1, 1)
                if n + 2 < NR:
                    quant_w(n + 2)
                if n % 2 == 0 and 0 <= (n - 4) // 2 < NI:
                    emb_t((n - 4) // 2)
                if emb:
                    out_score(i)
                    out_emb(i)
                if n in (1, 2):
                    pgs.append(p_half(1, n - 1))
                if n in (2, 3):
                    quant_p(1, n - 2, pgs[n])
                if n + 3 < NR:
                    inter_w(n + 3)
            nc.sync.dma_start(out=out_1.rearrange("(st r) c -> r st c", r=P), in_=score[:])
